import numpy as np
import ml_dtypes


def mxq(x, axis, fmt="e4m3"):
    dtype, down = {"e4m3": (ml_dtypes.float8_e4m3fn, 7), "e5m2": (ml_dtypes.float8_e5m2, 14)}[fmt]
    v = np.moveaxis(np.asarray(x, np.float32).astype(ml_dtypes.bfloat16).astype(np.float64), axis, -1)
    blocks = v.reshape(v.shape[:-1] + (-1, 32))
    amax = np.abs(blocks).max(-1, keepdims=True)
    byte = np.maximum(np.where(amax > 0, np.frexp(amax)[1] - 1 + 127, 0) - down, 1)
    scale = np.exp2(byte - 127.0)
    codes = (blocks / scale).astype(np.float32).astype(dtype).astype(np.float64)
    return np.moveaxis((codes * scale).reshape(v.shape), -1, axis)


WIDE = False


def mx_kscale(k):
    if not WIDE:
        return np.ones(k)
    levels = np.array([10, -10, 5, -5, 0])
    if k % 512:
        return np.exp2(np.random.permutation(np.resize(levels, k // 32))).repeat(32)
    a = np.empty((k // 512, 16))
    for p in range(k // 512):
        a[p, :8] = np.random.permutation(np.resize(levels, 8))
        for g in range(8):
            far = levels[np.abs(levels - a[p, g]) >= 10]
            a[p, g + 8] = far[np.random.randint(len(far))]
    return np.exp2(a.ravel()).repeat(32)


def f64(x):
    return np.asarray(x).astype(np.float64)


def striped(idx):
    return np.tile(idx.reshape(-1, 16).T, (8, 1)).astype(np.uint16)


def unstriped(offs):
    return offs[:16].T.reshape(-1).astype(np.int64)


E2M1 = np.array([0.0, 0.5, 1.0, 1.5, 2.0, 3.0, 4.0, 6.0, -0.0, -0.5, -1.0, -1.5, -2.0, -3.0, -4.0, -6.0])


def pack_weight(w, fmt):
    k, n = w.shape
    w = f64(np.asarray(w, np.float32).astype(ml_dtypes.bfloat16)).reshape(k // 32, 32, n)
    amax = np.abs(w).max(1)
    if fmt == "e4m3":
        byte = np.frexp(amax)[1] - 1 + 127 - 7
    else:
        mant, ex = np.frexp(amax / 6.0)
        byte = np.where(mant > 0.5, ex, ex - 1) + 127
    byte = np.clip(np.where(amax > 0, byte, 1), 1, 254)
    scaled = (w * np.exp2(127.0 - byte)[:, None, :]).reshape(k, n).astype(np.float32)
    by_word = np.ascontiguousarray(scaled.reshape(k // 512, 128, 4, n).transpose(0, 1, 3, 2))
    if fmt == "e4m3":
        words = by_word.astype(ml_dtypes.float8_e4m3fn).view(np.uint8)
    else:
        c = by_word.astype(ml_dtypes.float4_e2m1fn).view(np.uint8) & 0xF
        words = (c[..., 0::2] | (c[..., 1::2] << 4)).reshape(k // 512, 128, 2 * n)
    return np.ascontiguousarray(words), np.ascontiguousarray(byte.astype(np.uint8).reshape(k // 512, 16, n))


def unpack_weight(words, scales, fmt):
    g, _, n = scales.shape
    words = np.ascontiguousarray(words).reshape(g, 128, n, -1)
    if fmt == "e4m3":
        vals = words.view(ml_dtypes.float8_e4m3fn).astype(np.float64)
    else:
        nib = np.empty((g, 128, n, 4), np.uint8)
        nib[..., 0::2] = words & 0xF
        nib[..., 1::2] = words >> 4
        vals = E2M1[nib]
    vals = vals * np.repeat(np.exp2(scales.astype(np.float64) - 127.0), 8, axis=1)[..., None]
    return vals.transpose(0, 1, 3, 2).reshape(g * 512, n)


def gelu(v):
    return 0.5 * v * (1.0 + np.tanh(np.sqrt(2.0 / np.pi) * (v + 0.044715 * v**3)))


def striped8(idx):
    return np.concatenate([v.reshape(-1, 16).T for v in idx]).astype(np.uint16)


def unstriped8(offs):
    return np.stack([offs[16 * g:16 * g + 16].T.reshape(-1) for g in range(8)]).astype(np.int64)


def heads(h, wgt, idx8):
    r = np.arange(h.shape[0])
    return wgt[r // 4 % 128] * h[r[:, None], idx8[r % 512 // 64]]


K, T, S, H, P, N = 512, 4096, 2048, 1024, 1024, 768

def setup_inputs():
    n = np.random.standard_normal
    s = mx_kscale(K)[:, None]
    u = mx_kscale(H)[:, None]
    tab_words, tab_scales = pack_weight(n((K, T)) * s, "e4m3")
    w4_words, w4_scales = pack_weight(0.8 * n((K, H)) / np.sqrt(K) / s, "e2m1")
    return {
        "tab_words": tab_words, "tab_scales": tab_scales,
        "offs": striped(np.random.permutation(T)[:S]),
        "offs2": striped8(np.stack([np.random.permutation(S)[:P] for _ in range(8)])),
        "offs3": striped8(np.stack([np.random.permutation(S)[:P] for _ in range(8)])),
        "w1": (0.8 * n((K, H)) / np.sqrt(K) / s).astype(np.float32),
        "b1": (0.4 * n(H)).astype(np.float32),
        "w4_words": w4_words, "w4_scales": w4_scales,
        "b4": (0.4 * n(H)).astype(np.float32),
        "wga": np.repeat(np.random.uniform(0.5, 2.0, (8, P)), 16, axis=0).astype(np.float32),
        "wgb": np.repeat(np.random.uniform(0.5, 2.0, (8, P)), 16, axis=0).astype(np.float32),
        "gain": (0.7 * np.exp(0.3 * n(H)) * u[:, 0]).astype(np.float32),
        "w2": (n((H, N)) / np.sqrt(H) / u).astype(np.float32),
        "b2": (0.4 * n(N)).astype(np.float32),
    }

def reference(tab_words, tab_scales, offs, offs2, offs3, w1, b1, w4_words, w4_scales, b4,
              wga, wgb, gain, w2, b2):
    v = unpack_weight(tab_words, tab_scales, "e4m3")[:, unstriped(offs)]
    w4 = unpack_weight(w4_words, w4_scales, "e2m1")
    he = (mxq(f64(w1), 0, "e4m3").T @ v) + f64(b1)[:, None]
    hj = (w4.T @ v) + f64(b4)[:, None]
    xa = heads(he, f64(wga), unstriped8(offs2))
    xb = heads(hj, f64(wgb), unstriped8(offs3))
    top = np.maximum(xa, xb)
    z = f64(gain)[:, None] * (top * xb)
    y = (mxq(f64(w2), 0, "e4m3").T @ mxq(z, 0, "e4m3")) + f64(b2)[:, None]
    return np.abs(y)

@@ -1,0 +1,249 @@
+from contextlib import ExitStack
+
+import concourse.mybir as mybir
+
+K, T, S, H, M, N = 512, 4096, 2048, 1024, 1024, 768
+FLOPS = 2 * (2 * K * H * S + H * N * M)
+
+F32 = mybir.dt.float32
+BF16 = mybir.dt.bfloat16
+I32 = mybir.dt.int32
+U32 = mybir.dt.uint32
+U16 = mybir.dt.uint16
+U8 = mybir.dt.uint8
+FP8X4 = mybir.dt.float8_e4m3fn_x4
+FP4X4 = mybir.dt.float4_e2m1fn_x4
+ALU = mybir.AluOpType
+ACT = mybir.ActivationFunctionType
+
+P = 128
+PACK = 4
+PASS = P * PACK
+BANK = 512
+PER_COL = 16
+RUN = 4
+AREA_WORDS, AREA_SCALES, AREA_W4 = 0, 16384, 29696
+AREA_PICKED = 34304
+TAIL_PIECES = (256, 256, 256, 128, 128)
+
+
+def tile_list_roost_jamming_scores_kernel(
+    tc, tab_words, tab_scales, offs, offs2, offs3, w1, b1, w4_words, w4_scales, b4,
+    wga, wgb, gain, w2, b2, out,
+):
+    nc = tc.nc
+    with ExitStack() as ctx:
+        keep = ctx.enter_context(tc.tile_pool(name="keep", bufs=1))
+        reuse = ctx.enter_context(tc.tile_pool(name="reuse", bufs=1))
+        ring = ctx.enter_context(tc.tile_pool(name="ring", bufs=2))
+        psum = ctx.enter_context(tc.psum_pool(name="psum", bufs=8))
+
+        def load_scale_rows(dst, src, engine, queue):
+            engine.memset(dst[:].bitcast(I32), 0)
+            for q in range(4):
+                queue.dma_start(dst[32 * q : 32 * q + 4, :].bitcast(I32), src[0, 4 * q : 4 * q + 4, :].bitcast(I32))
+
+        list1 = keep.tile([P, S // PER_COL], U16, name="list1")
+        list2 = keep.tile([P, M // PER_COL], U16, name="list2")
+        list3 = keep.tile([P, M // PER_COL], U16, name="list3")
+        tab_w = reuse.tile([P, T], U32, name="tab_w", align_bytes=64, offset=AREA_WORDS)
+        tab_s = reuse.tile([P, T], U8, name="tab_s", align_bytes=64, offset=AREA_SCALES)
+        w4_raw = reuse.tile([P, H], U16, name="w4_raw", align_bytes=64, offset=AREA_W4)
+        w4s_raw = reuse.tile([P, H], U8, name="w4s_raw", align_bytes=64, offset=AREA_PICKED + 4 * BANK)
+        nc.sync.dma_start(list1[:], offs)
+        load_scale_rows(tab_s, tab_scales, nc.vector, nc.sync)
+        nc.sync.dma_start(list3[:], offs3)
+        nc.sync.dma_start(list2[:], offs2)
+        nc.sync.dma_start(tab_w[:].bitcast(I32), tab_words[0].rearrange("p t i -> p (t i)").bitcast(I32))
+        load_scale_rows(w4s_raw, w4_scales, nc.gpsimd, nc.gpsimd)
+        nc.sync.dma_start(w4_raw[:].bitcast(I32), w4_words[0].bitcast(I32))
+
+        def load_per_row(name, vec, offset):
+            dst = reuse.tile([P, H // P], F32, name=name, align_bytes=64, offset=offset)
+            nc.sync.dma_start(dst[:].rearrange("p (b i) -> p b i", i=PACK), vec.rearrange("(b p i) -> p b i", p=P, i=PACK))
+            return dst
+
+        def load_weight(name, rows, offset):
+            raw = reuse.tile([P, PACK, rows.shape[1]], F32, name=name, align_bytes=64, offset=offset)
+            nc.sync.dma_start(raw[:], rows.rearrange("(p j) c -> p j c", j=PACK))
+            return raw
+
+        v_s = keep.tile([P, S], U8, name="v_s", align_bytes=64)
+        nc.vector.tensor_copy(v_s[:], tab_s[:].indirect(list1[:]))
+
+        w4_w = keep.tile([P, H], U16, name="w4_w", align_bytes=64)
+        w4_s = reuse.tile([P, H], U8, name="w4_s", align_bytes=64, offset=AREA_SCALES)
+
+        def deal_w4(copy, dst, src, b):
+            cols = slice(b * PASS, (b + 1) * PASS)
+            copy(dst[:, cols].rearrange("p (i m) -> p i m", i=PACK), src[:, cols].rearrange("p (m i) -> p i m", i=PACK))
+
+        for b in range(2):
+            deal_w4(nc.vector.tensor_copy, w4_s, w4s_raw, b)
+            deal_w4(nc.scalar.copy, w4_w, w4_raw, b)
+        b4_sb = load_per_row("b4_sb", b4, AREA_W4)
+        wgb_sb = reuse.tile([P, M], F32, name="wgb_sb", align_bytes=64, offset=AREA_W4 + 256)
+        nc.sync.dma_start(wgb_sb[:], wgb)
+        w1_raw = [load_weight("w1_raw0", w1[:, 0:PASS], AREA_SCALES + H)]
+        b1_sb = load_per_row("b1_sb", b1, AREA_W4 + 64)
+        gain_sb = load_per_row("gain_sb", gain, AREA_W4 + 128)
+        b2_sb = reuse.tile([P, N // P], F32, name="b2_sb", align_bytes=64, offset=AREA_W4 + 192)
+        with nc.allow_non_contiguous_dma(reason="one bias value a partition"):
+            nc.sync.dma_start(b2_sb[:], b2.rearrange("(c p) -> p c", p=P))
+        v_w = []
+        for c in range(S // BANK):
+            v_w.append(reuse.tile([P, BANK], U32, name=f"v_w{c}", align_bytes=64, offset=AREA_PICKED + 4 * BANK * c))
+            nc.vector.tensor_copy(
+                v_w[c][:],
+                tab_w[:].indirect(list1[:, c * BANK // PER_COL : (c + 1) * BANK // PER_COL]),
+            )
+
+        wga_sb = reuse.tile([P, M], F32, name="wga_sb", align_bytes=64, offset=AREA_WORDS)
+        nc.sync.dma_start(wga_sb[:], wga)
+        w1_raw.append(load_weight("w1_raw1", w1[:, PASS : 2 * PASS], AREA_WORDS + 4096))
+        w1_w = keep.tile([P, H], U32, name="w1_w", align_bytes=64)
+        w1_s = keep.tile([P, H], U8, name="w1_s", align_bytes=64)
+
+        def quantise_w1(b, u, copy):
+            grouped = ring.tile([P, 2, P, PACK], BF16, name="grouped", tag="grouped", bufs=3, align_bytes=64)
+            copy(
+                grouped[:].rearrange("p i m j -> p m j i"),
+                w1_raw[b][:].rearrange("p j (m i) -> p m j i", i=PACK)[:, :, :, 2 * u : 2 * u + 2],
+            )
+            cols = slice(b * PASS + 2 * u * P, b * PASS + (2 * u + 2) * P)
+            nc.vector.quantize_mx(
+                out=w1_w[:, cols].bitcast(FP8X4), scales=w1_s[:, cols],
+                in_=grouped[:].rearrange("p i m j -> p (i m j)"),
+            )
+
+        def feature_chunk(h, side, row, c):
+            w_codes, w_scales, dtype, bias = side
+            cols = slice(row * P, (row + 1) * P)
+            picked = slice(c * BANK, (c + 1) * BANK)
+            acc = psum.tile([P, BANK], F32, name="acc", tag="acc")
+            nc.tensor.matmul_mx(
+                out=acc[:], lhsT=w_codes[:, cols].bitcast(dtype), lhsT_scale=w_scales[:, cols],
+                rhs=v_w[c][:].bitcast(FP8X4), rhs_scale=v_s[:, picked], start=True, stop=True,
+            )
+            nc.scalar.activation(out=h[:, picked], in_=acc[:], func=ACT.Identity, bias=bias[:, row : row + 1])
+
+        def features(side, some_rows):
+            tiles = [ring.tile([P, S], F32, name="h", tag="h", bufs=8) for row in some_rows]
+            for c in range(S // BANK):
+                for h, row in zip(tiles, some_rows):
+                    feature_chunk(h, side, row, c)
+            return tiles
+
+        jammer = (w4_w, w4_s, FP4X4, b4_sb)
+        emitter = (w1_w, w1_s, FP8X4, b1_sb)
+
+        def pick(dst, h, lst, wg, m0, m1):
+            nc.vector.tensor_tensor(
+                dst, h[:].indirect(lst[:, m0 // PER_COL : m1 // PER_COL]), wg[:, m0:m1], ALU.mult
+            )
+
+        z_planes = [
+            keep.tile([P, PACK, M], BF16, name=f"z_planes{b}", align_bytes=64) for b in range(2)
+        ]
+
+        def combine(jobs):
+            for top, xa, xb, row, m0, m1 in jobs:
+                nc.vector.tensor_tensor(top, xa, xb, ALU.max)
+            for top, xa, xb, row, m0, m1 in jobs:
+                nc.vector.scalar_tensor_tensor(
+                    z_planes[row // PACK][:, row % PACK, m0:m1], top, gain_sb[:, row : row + 1], xb, ALU.mult, ALU.mult
+                )
+
+        def whole_row(row, hj, he):
+            xb = ring.tile([P, M], F32, name="xb", tag="xb", bufs=2)
+            xa = ring.tile([P, M], F32, name="xa", tag="xa", bufs=2)
+            pick(xb[:], hj, list3, wgb_sb, 0, M)
+            halves = [(0, M // 2), (M // 2, M)]
+            for m0, m1 in halves:
+                pick(xa[:, m0:m1], he, list2, wga_sb, m0, m1)
+            combine([(xa[:, m0:m1], xa[:, m0:m1], xb[:, m0:m1], row, m0, m1) for m0, m1 in halves])
+
+        z_w = [keep.tile([P, M], U32, name=f"z_w{b}", align_bytes=64) for b in range(2)]
+        z_s = [keep.tile([P, M], U8, name=f"z_s{b}", align_bytes=64) for b in range(2)]
+
+        def interleave(dst, src):
+            nc.scalar.copy(
+                dst.rearrange("p (c i) j -> p c j i", i=RUN), src.rearrange("p j (c i) -> p c j i", i=RUN)
+            )
+
+        def quantise_planes(planes, grouped, codes, scales):
+            interleave(grouped[:], planes)
+            nc.vector.quantize_mx(
+                out=codes.bitcast(FP8X4), scales=scales, in_=grouped[:].rearrange("p c j -> p (c j)")
+            )
+
+        def quantise_z(b, m0, m1, grouped):
+            quantise_planes(z_planes[b][:, :, m0:m1], grouped, z_w[b][:, m0:m1], z_s[b][:, m0:m1])
+
+        w2_w = [keep.tile([P, N], U32, name=f"w2_w{b}", align_bytes=64) for b in range(2)]
+        w2_s = [keep.tile([P, N], U8, name=f"w2_s{b}", align_bytes=64) for b in range(2)]
+
+        def quantise_w2(b, half):
+            cols = slice(half * N // 2, (half + 1) * N // 2)
+            grouped = ring.tile([P, N // 2, PACK], BF16, name="grouped", tag="grouped", bufs=3, align_bytes=64)
+            quantise_planes(w2_raw[b][:, :, cols], grouped, w2_w[b][:, cols], w2_s[b][:, cols])
+
+        def scores(m0, m1):
+            staged = ring.tile([P, N // P, m1 - m0], F32, name="staged", tag="staged", bufs=3)
+            for c in range(N // P):
+                acc = psum.tile([P, m1 - m0], F32, name="acc", tag="acc")
+                cols = slice(c * P, (c + 1) * P)
+                for b in range(2):
+                    nc.tensor.matmul_mx(
+                        out=acc[:], lhsT=w2_w[b][:, cols].bitcast(FP8X4), lhsT_scale=w2_s[b][:, cols],
+                        rhs=z_w[b][:, m0:m1].bitcast(FP8X4), rhs_scale=z_s[b][:, m0:m1],
+                        start=(b == 0), stop=(b == 1),
+                    )
+                nc.scalar.activation(out=staged[:, c, :], in_=acc[:], func=ACT.Abs, bias=b2_sb[:, c : c + 1])
+            nc.sync.dma_start(out[:, m0:m1].rearrange("(c p) m -> p c m", p=P), staged[:])
+
+        rows = H // P
+        quantise_w1(0, 0, nc.vector.tensor_copy)
+        hj = features(jammer, [0, 1])
+        he = []
+        w2_raw = []
+        for row in range(rows):
+            if 1 <= row < rows - 1:
+                hj.extend(features(jammer, [row + 1]))
+            he.extend(features(emitter, [row]))
+            if row < PACK - 1:
+                quantise_w1((row + 1) // 2, (row + 1) % 2, nc.scalar.copy)
+            if row in (0, 2):
+                b = row // 2
+                w2_raw.append(
+                    load_weight(f"w2_raw{b}", w2[b * PASS : (b + 1) * PASS, :], (AREA_SCALES + H, AREA_WORDS + 4096)[b])
+                )
+            if row < rows - 2:
+                whole_row(row, hj[row], he[row])
+            if PACK - 1 <= row < rows - 1:
+                quantise_w2(*divmod(row - PACK + 1, 2))
+        for half in range(2):
+            grouped = reuse.tile(
+                [P, M // 2, PACK], BF16, name=f"z_grouped{half}", align_bytes=64, offset=AREA_PICKED + 4096 * (1 - half)
+            )
+            quantise_z(0, half * M // 2, (half + 1) * M // 2, grouped)
+
+        m0 = 0
+        before = None
+        for width in TAIL_PIECES:
+            m1 = m0 + width
+            xb = ring.tile([P, 2, width], F32, name="xb_tail", tag="xb_tail", bufs=1)
+            xa = ring.tile([P, 2, width], F32, name="xa_tail", tag="xa_tail", bufs=1)
+            top = ring.tile([P, 2, width], F32, name="top", tag="tail", bufs=1, align_bytes=64)
+            for t in range(2):
+                pick(xb[:, t, :], hj[rows - 2 + t], list3, wgb_sb, m0, m1)
+            for t in range(2):
+                pick(xa[:, t, :], he[rows - 2 + t], list2, wga_sb, m0, m1)
+            combine([(top[:, t, :], xa[:, t, :], xb[:, t, :], rows - 2 + t, m0, m1) for t in range(2)])
+            grouped = ring.tile([P, width, PACK], BF16, name="grouped_tail", tag="tail", bufs=1, align_bytes=64)
+            quantise_z(1, m0, m1, grouped)
+            if before is not None:
+                scores(*before)
+            before = (m0, m1)
+            m0 = m1
+        scores(*before)

@@ -22,8 +22,8 @@ PASS = P * PACK
 BANK = 512
 PER_COL = 16
 RUN = 4
-AREA_WORDS, AREA_SCALES, AREA_W4 = 0, 16384, 29696
-AREA_PICKED = 34304
+AREA_WORDS, AREA_SCALES, AREA_PICKED, AREA_W1 = 0, 16384, 29696, 37888
+H_SLOTS = 8
 TAIL_PIECES = (256, 256, 256, 128, 128)
 
 
@@ -36,30 +36,26 @@ def tile_list_roost_jamming_scores_kernel(
         keep = ctx.enter_context(tc.tile_pool(name="keep", bufs=1))
         reuse = ctx.enter_context(tc.tile_pool(name="reuse", bufs=1))
         ring = ctx.enter_context(tc.tile_pool(name="ring", bufs=2))
-        psum = ctx.enter_context(tc.psum_pool(name="psum", bufs=8))
+        psum = ctx.enter_context(tc.psum_pool(name="psum", bufs=1))
 
-        def load_scale_rows(dst, src, engine, queue):
+        banks_used = []
+
+        def next_bank(width):
+            banks_used.append(width)
+            return psum.tile([P, width], F32, name="acc", tag=f"bank{len(banks_used) % 8}")
+
+        def load_scale_rows(dst, src, engine):
             engine.memset(dst[:].bitcast(I32), 0)
             for q in range(4):
-                queue.dma_start(dst[32 * q : 32 * q + 4, :].bitcast(I32), src[0, 4 * q : 4 * q + 4, :].bitcast(I32))
+                nc.sync.dma_start(dst[32 * q : 32 * q + 4, :].bitcast(I32), src[0, 4 * q : 4 * q + 4, :].bitcast(I32))
 
-        list1 = keep.tile([P, S // PER_COL], U16, name="list1")
-        list2 = keep.tile([P, M // PER_COL], U16, name="list2")
-        list3 = keep.tile([P, M // PER_COL], U16, name="list3")
-        tab_w = reuse.tile([P, T], U32, name="tab_w", align_bytes=64, offset=AREA_WORDS)
-        tab_s = reuse.tile([P, T], U8, name="tab_s", align_bytes=64, offset=AREA_SCALES)
-        w4_raw = reuse.tile([P, H], U16, name="w4_raw", align_bytes=64, offset=AREA_W4)
-        w4s_raw = reuse.tile([P, H], U8, name="w4s_raw", align_bytes=64, offset=AREA_PICKED + 4 * BANK)
-        nc.sync.dma_start(list1[:], offs)
-        load_scale_rows(tab_s, tab_scales, nc.vector, nc.sync)
-        nc.sync.dma_start(list3[:], offs3)
-        nc.sync.dma_start(list2[:], offs2)
-        nc.sync.dma_start(tab_w[:].bitcast(I32), tab_words[0].rearrange("p t i -> p (t i)").bitcast(I32))
-        load_scale_rows(w4s_raw, w4_scales, nc.gpsimd, nc.gpsimd)
-        nc.sync.dma_start(w4_raw[:].bitcast(I32), w4_words[0].bitcast(I32))
+        def load_plain(name, src, dtype):
+            dst = keep.tile(list(src.shape), dtype, name=name)
+            nc.sync.dma_start(dst[:], src)
+            return dst
 
-        def load_per_row(name, vec, offset):
-            dst = reuse.tile([P, H // P], F32, name=name, align_bytes=64, offset=offset)
+        def load_per_row(name, vec):
+            dst = keep.tile([P, H // P], F32, name=name)
             nc.sync.dma_start(dst[:].rearrange("p (b i) -> p b i", i=PACK), vec.rearrange("(b p i) -> p b i", p=P, i=PACK))
             return dst
 
@@ -67,6 +63,28 @@ def tile_list_roost_jamming_scores_kernel(
             raw = reuse.tile([P, PACK, rows.shape[1]], F32, name=name, align_bytes=64, offset=offset)
             nc.sync.dma_start(raw[:], rows.rearrange("(p j) c -> p j c", j=PACK))
             return raw
+
+        tab_w = reuse.tile([P, T], U32, name="tab_w", align_bytes=64, offset=AREA_WORDS)
+        tab_s = reuse.tile([P, T], U8, name="tab_s", align_bytes=64, offset=AREA_SCALES)
+        w4_raw = keep.tile([P, H], U16, name="w4_raw", align_bytes=64)
+        w4s_raw = reuse.tile([P, H], U8, name="w4s_raw", align_bytes=64, offset=AREA_PICKED + 4 * BANK)
+        list1 = load_plain("list1", offs, U16)
+        load_scale_rows(tab_s, tab_scales, nc.vector)
+        list3 = load_plain("list3", offs3, U16)
+        list2 = load_plain("list2", offs2, U16)
+        nc.sync.dma_start(tab_w[:].bitcast(I32), tab_words[0].rearrange("p t i -> p (t i)").bitcast(I32))
+        load_scale_rows(w4s_raw, w4_scales, nc.gpsimd)
+        nc.sync.dma_start(w4_raw[:].bitcast(I32), w4_words[0].bitcast(I32))
+        b4_sb = load_per_row("b4_sb", b4)
+        w1_raw = [load_weight("w1_raw0", w1[:, 0:PASS], AREA_SCALES + T)]
+        wgb_sb = load_plain("wgb_sb", wgb, F32)
+        b1_sb = load_per_row("b1_sb", b1)
+        gain_sb = load_per_row("gain_sb", gain)
+        wga_sb = load_plain("wga_sb", wga, F32)
+        w1_raw.append(load_weight("w1_raw1", w1[:, PASS : 2 * PASS], AREA_W1))
+        b2_sb = keep.tile([P, N // P], F32, name="b2_sb")
+        with nc.allow_non_contiguous_dma(reason="one bias value a partition"):
+            nc.sync.dma_start(b2_sb[:], b2.rearrange("(c p) -> p c", p=P))
 
         v_s = keep.tile([P, S], U8, name="v_s", align_bytes=64)
         nc.vector.tensor_copy(v_s[:], tab_s[:].indirect(list1[:]))
@@ -81,15 +99,6 @@ def tile_list_roost_jamming_scores_kernel(
         for b in range(2):
             deal_w4(nc.vector.tensor_copy, w4_s, w4s_raw, b)
             deal_w4(nc.scalar.copy, w4_w, w4_raw, b)
-        b4_sb = load_per_row("b4_sb", b4, AREA_W4)
-        wgb_sb = reuse.tile([P, M], F32, name="wgb_sb", align_bytes=64, offset=AREA_W4 + 256)
-        nc.sync.dma_start(wgb_sb[:], wgb)
-        w1_raw = [load_weight("w1_raw0", w1[:, 0:PASS], AREA_SCALES + H)]
-        b1_sb = load_per_row("b1_sb", b1, AREA_W4 + 64)
-        gain_sb = load_per_row("gain_sb", gain, AREA_W4 + 128)
-        b2_sb = reuse.tile([P, N // P], F32, name="b2_sb", align_bytes=64, offset=AREA_W4 + 192)
-        with nc.allow_non_contiguous_dma(reason="one bias value a partition"):
-            nc.sync.dma_start(b2_sb[:], b2.rearrange("(c p) -> p c", p=P))
         v_w = []
         for c in range(S // BANK):
             v_w.append(reuse.tile([P, BANK], U32, name=f"v_w{c}", align_bytes=64, offset=AREA_PICKED + 4 * BANK * c))
@@ -98,14 +107,11 @@ def tile_list_roost_jamming_scores_kernel(
                 tab_w[:].indirect(list1[:, c * BANK // PER_COL : (c + 1) * BANK // PER_COL]),
             )
 
-        wga_sb = reuse.tile([P, M], F32, name="wga_sb", align_bytes=64, offset=AREA_WORDS)
-        nc.sync.dma_start(wga_sb[:], wga)
-        w1_raw.append(load_weight("w1_raw1", w1[:, PASS : 2 * PASS], AREA_WORDS + 4096))
         w1_w = keep.tile([P, H], U32, name="w1_w", align_bytes=64)
         w1_s = keep.tile([P, H], U8, name="w1_s", align_bytes=64)
 
         def quantise_w1(b, u, copy):
-            grouped = ring.tile([P, 2, P, PACK], BF16, name="grouped", tag="grouped", bufs=3, align_bytes=64)
+            grouped = keep.tile([P, 2, P, PACK], BF16, name=f"w1_grouped{b}{u}", align_bytes=64)
             copy(
                 grouped[:].rearrange("p i m j -> p m j i"),
                 w1_raw[b][:].rearrange("p j (m i) -> p m j i", i=PACK)[:, :, :, 2 * u : 2 * u + 2],
@@ -120,15 +126,20 @@ def tile_list_roost_jamming_scores_kernel(
             w_codes, w_scales, dtype, bias = side
             cols = slice(row * P, (row + 1) * P)
             picked = slice(c * BANK, (c + 1) * BANK)
-            acc = psum.tile([P, BANK], F32, name="acc", tag="acc")
+            acc = next_bank(BANK)
             nc.tensor.matmul_mx(
                 out=acc[:], lhsT=w_codes[:, cols].bitcast(dtype), lhsT_scale=w_scales[:, cols],
                 rhs=v_w[c][:].bitcast(FP8X4), rhs_scale=v_s[:, picked], start=True, stop=True,
             )
             nc.scalar.activation(out=h[:, picked], in_=acc[:], func=ACT.Identity, bias=bias[:, row : row + 1])
 
+        made = []
+
         def features(side, some_rows):
-            tiles = [ring.tile([P, S], F32, name="h", tag="h", bufs=8) for row in some_rows]
+            tiles = []
+            for row in some_rows:
+                tiles.append(keep.tile([P, S], F32, name="h", tag=f"h{len(made) % H_SLOTS}"))
+                made.append(row)
             for c in range(S // BANK):
                 for h, row in zip(tiles, some_rows):
                     feature_chunk(h, side, row, c)
@@ -155,8 +166,8 @@ def tile_list_roost_jamming_scores_kernel(
                 )
 
         def whole_row(row, hj, he):
-            xb = ring.tile([P, M], F32, name="xb", tag="xb", bufs=2)
-            xa = ring.tile([P, M], F32, name="xa", tag="xa", bufs=2)
+            xb = keep.tile([P, M], F32, name="xb", tag=f"xb{row % 2}")
+            xa = keep.tile([P, M], F32, name="xa", tag=f"xa{row % 2}")
             pick(xb[:], hj, list3, wgb_sb, 0, M)
             halves = [(0, M // 2), (M // 2, M)]
             for m0, m1 in halves:
@@ -185,13 +196,13 @@ def tile_list_roost_jamming_scores_kernel(
 
         def quantise_w2(b, half):
             cols = slice(half * N // 2, (half + 1) * N // 2)
-            grouped = ring.tile([P, N // 2, PACK], BF16, name="grouped", tag="grouped", bufs=3, align_bytes=64)
+            grouped = keep.tile([P, N // 2, PACK], BF16, name=f"w2_grouped{b}{half}", align_bytes=64)
             quantise_planes(w2_raw[b][:, :, cols], grouped, w2_w[b][:, cols], w2_s[b][:, cols])
 
         def scores(m0, m1):
-            staged = ring.tile([P, N // P, m1 - m0], F32, name="staged", tag="staged", bufs=3)
+            staged = keep.tile([P, N // P, m1 - m0], F32, name=f"staged{m0}")
             for c in range(N // P):
-                acc = psum.tile([P, m1 - m0], F32, name="acc", tag="acc")
+                acc = next_bank(m1 - m0)
                 cols = slice(c * P, (c + 1) * P)
                 for b in range(2):
                     nc.tensor.matmul_mx(
@@ -216,7 +227,7 @@ def tile_list_roost_jamming_scores_kernel(
             if row in (0, 2):
                 b = row // 2
                 w2_raw.append(
-                    load_weight(f"w2_raw{b}", w2[b * PASS : (b + 1) * PASS, :], (AREA_SCALES + H, AREA_WORDS + 4096)[b])
+                    load_weight(f"w2_raw{b}", w2[b * PASS : (b + 1) * PASS, :], (AREA_WORDS, AREA_SCALES + H)[b])
                 )
             if row < rows - 2:
                 whole_row(row, hj[row], he[row])

@@ -22,9 +22,11 @@ PASS = P * PACK
 BANK = 512
 PER_COL = 16
 RUN = 4
-AREA_WORDS, AREA_SCALES, AREA_PICKED, AREA_W1 = 0, 16384, 29696, 37888
+AREA_WORDS, AREA_SCALES, AREA_PICKED, AREA_W1 = 0, 16384, 29824, 38016
 H_SLOTS = 8
-TAIL_PIECES = (256, 256, 256, 128, 128)
+ROWS = H // P
+PAIR = 2
+TAIL_PIECES = ((256, 2), (256, 2), (256, 2), (128, 3), (128, 1))
 
 
 def tile_list_roost_jamming_scores_kernel(
@@ -35,7 +37,6 @@ def tile_list_roost_jamming_scores_kernel(
     with ExitStack() as ctx:
         keep = ctx.enter_context(tc.tile_pool(name="keep", bufs=1))
         reuse = ctx.enter_context(tc.tile_pool(name="reuse", bufs=1))
-        ring = ctx.enter_context(tc.tile_pool(name="ring", bufs=2))
         psum = ctx.enter_context(tc.psum_pool(name="psum", bufs=1))
 
         banks_used = []
@@ -54,10 +55,8 @@ def tile_list_roost_jamming_scores_kernel(
             nc.sync.dma_start(dst[:], src)
             return dst
 
-        def load_per_row(name, vec):
-            dst = keep.tile([P, H // P], F32, name=name)
+        def load_per_row(dst, vec):
             nc.sync.dma_start(dst[:].rearrange("p (b i) -> p b i", i=PACK), vec.rearrange("(b p i) -> p b i", p=P, i=PACK))
-            return dst
 
         def load_weight(name, rows, offset):
             raw = reuse.tile([P, PACK, rows.shape[1]], F32, name=name, align_bytes=64, offset=offset)
@@ -74,12 +73,15 @@ def tile_list_roost_jamming_scores_kernel(
         list2 = load_plain("list2", offs2, U16)
         nc.sync.dma_start(tab_w[:].bitcast(I32), tab_words[0].rearrange("p t i -> p (t i)").bitcast(I32))
         load_scale_rows(w4s_raw, w4_scales, nc.gpsimd)
+        gain_sb = keep.tile([P, ROWS], F32, name="gain_sb")
+        b4_sb = reuse.tile([P, ROWS], F32, name="b4_sb", align_bytes=64, offset=AREA_PICKED + 4 * BANK + H)
+        b1_sb = keep.tile([P, ROWS], F32, name="b1_sb")
         nc.sync.dma_start(w4_raw[:].bitcast(I32), w4_words[0].bitcast(I32))
-        b4_sb = load_per_row("b4_sb", b4)
+        load_per_row(gain_sb, gain)
+        load_per_row(b4_sb, b4)
         w1_raw = [load_weight("w1_raw0", w1[:, 0:PASS], AREA_SCALES + T)]
+        load_per_row(b1_sb, b1)
         wgb_sb = load_plain("wgb_sb", wgb, F32)
-        b1_sb = load_per_row("b1_sb", b1)
-        gain_sb = load_per_row("gain_sb", gain)
         wga_sb = load_plain("wga_sb", wga, F32)
         w1_raw.append(load_weight("w1_raw1", w1[:, PASS : 2 * PASS], AREA_W1))
         b2_sb = keep.tile([P, N // P], F32, name="b2_sb")
@@ -96,6 +98,14 @@ def tile_list_roost_jamming_scores_kernel(
             cols = slice(b * PASS, (b + 1) * PASS)
             copy(dst[:, cols].rearrange("p (i m) -> p i m", i=PACK), src[:, cols].rearrange("p (m i) -> p i m", i=PACK))
 
+        gain_sign = keep.tile([P, ROWS], F32, name="gain_sign")
+        gain_size = keep.tile([P, ROWS], F32, name="gain_size")
+        nc.scalar.activation(out=gain_sign[:], in_=gain_sb[:], func=ACT.Sign)
+        nc.scalar.activation(out=gain_size[:], in_=gain_sb[:], func=ACT.Abs)
+        b4_signed = reuse.tile([P, ROWS], F32, name="b4_signed", align_bytes=64, offset=AREA_SCALES + H)
+        b1_sized = reuse.tile([P, ROWS], F32, name="b1_sized", align_bytes=64, offset=AREA_SCALES + H + 64)
+        nc.vector.tensor_tensor(b4_signed[:], b4_sb[:], gain_sign[:], ALU.mult)
+        nc.vector.tensor_tensor(b1_sized[:], b1_sb[:], gain_size[:], ALU.mult)
         for b in range(2):
             deal_w4(nc.vector.tensor_copy, w4_s, w4s_raw, b)
             deal_w4(nc.scalar.copy, w4_w, w4_raw, b)
@@ -123,7 +133,7 @@ def tile_list_roost_jamming_scores_kernel(
             )
 
         def feature_chunk(h, side, row, c):
-            w_codes, w_scales, dtype, bias = side
+            w_codes, w_scales, dtype, factor, bias = side
             cols = slice(row * P, (row + 1) * P)
             picked = slice(c * BANK, (c + 1) * BANK)
             acc = next_bank(BANK)
@@ -131,7 +141,10 @@ def tile_list_roost_jamming_scores_kernel(
                 out=acc[:], lhsT=w_codes[:, cols].bitcast(dtype), lhsT_scale=w_scales[:, cols],
                 rhs=v_w[c][:].bitcast(FP8X4), rhs_scale=v_s[:, picked], start=True, stop=True,
             )
-            nc.scalar.activation(out=h[:, picked], in_=acc[:], func=ACT.Identity, bias=bias[:, row : row + 1])
+            nc.scalar.activation(
+                out=h[:, picked], in_=acc[:], func=ACT.Identity,
+                bias=bias[:, row : row + 1], scale=factor[:, row : row + 1],
+            )
 
         made = []
 
@@ -145,51 +158,32 @@ def tile_list_roost_jamming_scores_kernel(
                     feature_chunk(h, side, row, c)
             return tiles
 
-        jammer = (w4_w, w4_s, FP4X4, b4_sb)
-        emitter = (w1_w, w1_s, FP8X4, b1_sb)
+        jammer = (w4_w, w4_s, FP4X4, gain_sign, b4_signed)
+        emitter = (w1_w, w1_s, FP8X4, gain_size, b1_sized)
 
         def pick(dst, h, lst, wg, m0, m1):
             nc.vector.tensor_tensor(
                 dst, h[:].indirect(lst[:, m0 // PER_COL : m1 // PER_COL]), wg[:, m0:m1], ALU.mult
             )
 
-        z_planes = [
-            keep.tile([P, PACK, M], BF16, name=f"z_planes{b}", align_bytes=64) for b in range(2)
-        ]
-
-        def combine(jobs):
-            for top, xa, xb, row, m0, m1 in jobs:
-                nc.vector.tensor_tensor(top, xa, xb, ALU.max)
-            for top, xa, xb, row, m0, m1 in jobs:
-                nc.vector.scalar_tensor_tensor(
-                    z_planes[row // PACK][:, row % PACK, m0:m1], top, gain_sb[:, row : row + 1], xb, ALU.mult, ALU.mult
-                )
-
-        def whole_row(row, hj, he):
-            xb = keep.tile([P, M], F32, name="xb", tag=f"xb{row % 2}")
-            xa = keep.tile([P, M], F32, name="xa", tag=f"xa{row % 2}")
-            pick(xb[:], hj, list3, wgb_sb, 0, M)
-            halves = [(0, M // 2), (M // 2, M)]
-            for m0, m1 in halves:
-                pick(xa[:, m0:m1], he, list2, wga_sb, m0, m1)
-            combine([(xa[:, m0:m1], xa[:, m0:m1], xb[:, m0:m1], row, m0, m1) for m0, m1 in halves])
+        def larger(top, xa, xb, row):
+            nc.vector.scalar_tensor_tensor(top, xb, gain_sb[:, row : row + 1], xa, ALU.mult, ALU.max)
 
         z_w = [keep.tile([P, M], U32, name=f"z_w{b}", align_bytes=64) for b in range(2)]
         z_s = [keep.tile([P, M], U8, name=f"z_s{b}", align_bytes=64) for b in range(2)]
 
-        def interleave(dst, src):
-            nc.scalar.copy(
-                dst.rearrange("p (c i) j -> p c j i", i=RUN), src.rearrange("p j (c i) -> p c j i", i=RUN)
-            )
-
-        def quantise_planes(planes, grouped, codes, scales):
-            interleave(grouped[:], planes)
+        def quantise(grouped, codes, scales):
             nc.vector.quantize_mx(
                 out=codes.bitcast(FP8X4), scales=scales, in_=grouped[:].rearrange("p c j -> p (c j)")
             )
 
-        def quantise_z(b, m0, m1, grouped):
-            quantise_planes(z_planes[b][:, :, m0:m1], grouped, z_w[b][:, m0:m1], z_s[b][:, m0:m1])
+        def multiply(grouped, top, xb, m0, m1):
+            nc.vector.tensor_tensor(
+                grouped[:].rearrange("p (c i) j -> p c j i", i=PAIR),
+                top[:, :, m0:m1].rearrange("p j (c i) -> p c j i", i=PAIR),
+                xb[:, :, m0:m1].rearrange("p j (c i) -> p c j i", i=PAIR),
+                ALU.mult,
+            )
 
         w2_w = [keep.tile([P, N], U32, name=f"w2_w{b}", align_bytes=64) for b in range(2)]
         w2_s = [keep.tile([P, N], U8, name=f"w2_s{b}", align_bytes=64) for b in range(2)]
@@ -197,64 +191,85 @@ def tile_list_roost_jamming_scores_kernel(
         def quantise_w2(b, half):
             cols = slice(half * N // 2, (half + 1) * N // 2)
             grouped = keep.tile([P, N // 2, PACK], BF16, name=f"w2_grouped{b}{half}", align_bytes=64)
-            quantise_planes(w2_raw[b][:, :, cols], grouped, w2_w[b][:, cols], w2_s[b][:, cols])
+            nc.scalar.copy(
+                grouped[:].rearrange("p (c i) j -> p c j i", i=RUN),
+                w2_raw[b][:, :, cols].rearrange("p j (c i) -> p c j i", i=RUN),
+            )
+            quantise(grouped, w2_w[b][:, cols], w2_s[b][:, cols])
 
-        def scores(m0, m1):
-            staged = keep.tile([P, N // P, m1 - m0], F32, name=f"staged{m0}")
-            for c in range(N // P):
-                acc = next_bank(m1 - m0)
-                cols = slice(c * P, (c + 1) * P)
+        def scores(m0, m1, per_bank):
+            width = m1 - m0
+            staged = keep.tile([P, N // P, width], F32, name=f"staged{m0}")
+            for c0 in range(0, N // P, per_bank):
+                acc = next_bank(per_bank * width)
                 for b in range(2):
-                    nc.tensor.matmul_mx(
-                        out=acc[:], lhsT=w2_w[b][:, cols].bitcast(FP8X4), lhsT_scale=w2_s[b][:, cols],
-                        rhs=z_w[b][:, m0:m1].bitcast(FP8X4), rhs_scale=z_s[b][:, m0:m1],
-                        start=(b == 0), stop=(b == 1),
+                    for k in range(per_bank):
+                        cols = slice((c0 + k) * P, (c0 + k + 1) * P)
+                        nc.tensor.matmul_mx(
+                            out=acc[:, k * width : (k + 1) * width],
+                            lhsT=w2_w[b][:, cols].bitcast(FP8X4), lhsT_scale=w2_s[b][:, cols],
+                            rhs=z_w[b][:, m0:m1].bitcast(FP8X4), rhs_scale=z_s[b][:, m0:m1],
+                            start=(b == 0 and k == 0), stop=(b == 1 and k == per_bank - 1),
+                        )
+                for k in range(per_bank):
+                    nc.scalar.activation(
+                        out=staged[:, c0 + k, :], in_=acc[:, k * width : (k + 1) * width],
+                        func=ACT.Abs, bias=b2_sb[:, c0 + k : c0 + k + 1],
                     )
-                nc.scalar.activation(out=staged[:, c, :], in_=acc[:], func=ACT.Abs, bias=b2_sb[:, c : c + 1])
             nc.sync.dma_start(out[:, m0:m1].rearrange("(c p) m -> p c m", p=P), staged[:])
 
-        rows = H // P
         quantise_w1(0, 0, nc.vector.tensor_copy)
         hj = features(jammer, [0, 1])
         he = []
         w2_raw = []
-        for row in range(rows):
-            if 1 <= row < rows - 1:
+        halves = [(0, M // 2), (M // 2, M)]
+        for row in range(ROWS):
+            b, i = divmod(row, PACK)
+            if 1 <= row < ROWS - 1:
                 hj.extend(features(jammer, [row + 1]))
             he.extend(features(emitter, [row]))
             if row < PACK - 1:
                 quantise_w1((row + 1) // 2, (row + 1) % 2, nc.scalar.copy)
             if row in (0, 2):
-                b = row // 2
+                half = row // 2
                 w2_raw.append(
-                    load_weight(f"w2_raw{b}", w2[b * PASS : (b + 1) * PASS, :], (AREA_WORDS, AREA_SCALES + H)[b])
+                    load_weight(
+                        f"w2_raw{half}", w2[half * PASS : (half + 1) * PASS, :], (AREA_WORDS, AREA_SCALES + H + 128)[half]
+                    )
                 )
-            if row < rows - 2:
-                whole_row(row, hj[row], he[row])
-            if PACK - 1 <= row < rows - 1:
+            if i == 0:
+                xb = keep.tile([P, PACK, M], F32, name="xb", tag="xb")
+                top = keep.tile([P, PACK, M], F32, name="top", tag="top")
+            pick(xb[:, i, :], hj[row], list3, wgb_sb, 0, M)
+            if row < ROWS - 2:
+                xa = keep.tile([P, M], F32, name="xa", tag="xa")
+                for m0, m1 in halves:
+                    pick(xa[:, m0:m1], he[row], list2, wga_sb, m0, m1)
+                for m0, m1 in halves:
+                    larger(top[:, i, m0:m1], xa[:, m0:m1], xb[:, i, m0:m1], row)
+            if row == PACK - 1:
+                grouped = [
+                    reuse.tile([P, M // 2, PACK], BF16, name=f"z_grouped{m0}", align_bytes=64, offset=AREA_W1 + 8 * m0)
+                    for m0, m1 in halves
+                ]
+                for tile, (m0, m1) in zip(grouped, halves):
+                    multiply(tile, top, xb, m0, m1)
+                for tile, (m0, m1) in zip(grouped, halves):
+                    quantise(tile, z_w[0][:, m0:m1], z_s[0][:, m0:m1])
+            if PACK - 1 <= row < ROWS - 1:
                 quantise_w2(*divmod(row - PACK + 1, 2))
-        for half in range(2):
-            grouped = reuse.tile(
-                [P, M // 2, PACK], BF16, name=f"z_grouped{half}", align_bytes=64, offset=AREA_PICKED + 4096 * (1 - half)
-            )
-            quantise_z(0, half * M // 2, (half + 1) * M // 2, grouped)
 
         m0 = 0
-        before = None
-        for width in TAIL_PIECES:
+        for width, per_bank in TAIL_PIECES:
             m1 = m0 + width
-            xb = ring.tile([P, 2, width], F32, name="xb_tail", tag="xb_tail", bufs=1)
-            xa = ring.tile([P, 2, width], F32, name="xa_tail", tag="xa_tail", bufs=1)
-            top = ring.tile([P, 2, width], F32, name="top", tag="tail", bufs=1, align_bytes=64)
-            for t in range(2):
-                pick(xb[:, t, :], hj[rows - 2 + t], list3, wgb_sb, m0, m1)
-            for t in range(2):
-                pick(xa[:, t, :], he[rows - 2 + t], list2, wga_sb, m0, m1)
-            combine([(top[:, t, :], xa[:, t, :], xb[:, t, :], rows - 2 + t, m0, m1) for t in range(2)])
-            grouped = ring.tile([P, width, PACK], BF16, name="grouped_tail", tag="tail", bufs=1, align_bytes=64)
-            quantise_z(1, m0, m1, grouped)
-            if before is not None:
-                scores(*before)
-            before = (m0, m1)
+            last_rows = range(ROWS - 2, ROWS)
+            xa = {row: keep.tile([P, width], F32, name="xa_tail", tag=f"xa_tail{row}") for row in last_rows}
+            for row in last_rows:
+                pick(xa[row][:], he[row], list2, wga_sb, m0, m1)
+            for row in last_rows:
+                larger(top[:, row % PACK, m0:m1], xa[row][:], xb[:, row % PACK, m0:m1], row)
+            tile = reuse.tile([P, width, PACK], BF16, name=f"z_tail{m0}", align_bytes=64, offset=AREA_W1 + 8 * m0)
+            multiply(tile, top, xb, m0, m1)
+            quantise(tile, z_w[1][:, m0:m1], z_s[1][:, m0:m1])
+            scores(m0, m1, per_bank)
             m0 = m1
-        scores(*before)

@@ -26,7 +26,7 @@ AREA_WORDS, AREA_SCALES, AREA_PICKED, AREA_W1 = 0, 16384, 29824, 38016
 H_SLOTS = 8
 ROWS = H // P
 PAIR = 2
-TAIL_PIECES = ((256, 2), (256, 2), (256, 2), (128, 3), (128, 1))
+TAIL_PIECES = ((256, 2, 6), (256, 2, 6), (256, 2, 6), (128, 3, 6), (128, 1, 2))
 
 
 def tile_list_roost_jamming_scores_kernel(
@@ -109,13 +109,11 @@ def tile_list_roost_jamming_scores_kernel(
         for b in range(2):
             deal_w4(nc.vector.tensor_copy, w4_s, w4s_raw, b)
             deal_w4(nc.scalar.copy, w4_w, w4_raw, b)
-        v_w = []
+        v_first = reuse.tile([P, BANK], U32, name="v_first", align_bytes=64, offset=AREA_PICKED)
+        v_rest = reuse.tile([P, S - BANK], U32, name="v_rest", align_bytes=64, offset=AREA_PICKED + 4 * BANK)
+        v_w = [v_first[:]] + [v_rest[:, c : c + BANK] for c in range(0, S - BANK, BANK)]
         for c in range(S // BANK):
-            v_w.append(reuse.tile([P, BANK], U32, name=f"v_w{c}", align_bytes=64, offset=AREA_PICKED + 4 * BANK * c))
-            nc.vector.tensor_copy(
-                v_w[c][:],
-                tab_w[:].indirect(list1[:, c * BANK // PER_COL : (c + 1) * BANK // PER_COL]),
-            )
+            nc.vector.tensor_copy(v_w[c], tab_w[:].indirect(list1[:, c * BANK // PER_COL : (c + 1) * BANK // PER_COL]))
 
         w1_w = keep.tile([P, H], U32, name="w1_w", align_bytes=64)
         w1_s = keep.tile([P, H], U8, name="w1_s", align_bytes=64)
@@ -139,7 +137,7 @@ def tile_list_roost_jamming_scores_kernel(
             acc = next_bank(BANK)
             nc.tensor.matmul_mx(
                 out=acc[:], lhsT=w_codes[:, cols].bitcast(dtype), lhsT_scale=w_scales[:, cols],
-                rhs=v_w[c][:].bitcast(FP8X4), rhs_scale=v_s[:, picked], start=True, stop=True,
+                rhs=v_w[c].bitcast(FP8X4), rhs_scale=v_s[:, picked], start=True, stop=True,
             )
             nc.scalar.activation(
                 out=h[:, picked], in_=acc[:], func=ACT.Identity,
@@ -197,7 +195,7 @@ def tile_list_roost_jamming_scores_kernel(
             )
             quantise(grouped, w2_w[b][:, cols], w2_s[b][:, cols])
 
-        def scores(m0, m1, per_bank):
+        def scores(m0, m1, per_bank, per_store):
             width = m1 - m0
             staged = keep.tile([P, N // P, width], F32, name=f"staged{m0}")
             for c0 in range(0, N // P, per_bank):
@@ -216,7 +214,12 @@ def tile_list_roost_jamming_scores_kernel(
                         out=staged[:, c0 + k, :], in_=acc[:, k * width : (k + 1) * width],
                         func=ACT.Abs, bias=b2_sb[:, c0 + k : c0 + k + 1],
                     )
-            nc.sync.dma_start(out[:, m0:m1].rearrange("(c p) m -> p c m", p=P), staged[:])
+                done = c0 + per_bank
+                if done % per_store == 0:
+                    first = done - per_store
+                    nc.sync.dma_start(
+                        out[first * P : done * P, m0:m1].rearrange("(c p) m -> p c m", p=P), staged[:, first:done, :]
+                    )
 
         quantise_w1(0, 0, nc.vector.tensor_copy)
         hj = features(jammer, [0, 1])
@@ -256,11 +259,13 @@ def tile_list_roost_jamming_scores_kernel(
                     multiply(tile, top, xb, m0, m1)
                 for tile, (m0, m1) in zip(grouped, halves):
                     quantise(tile, z_w[0][:, m0:m1], z_s[0][:, m0:m1])
-            if PACK - 1 <= row < ROWS - 1:
-                quantise_w2(*divmod(row - PACK + 1, 2))
+            if row in (PACK - 1, PACK):
+                quantise_w2(0, row - PACK + 1)
+        for half in range(2):
+            quantise_w2(1, half)
 
         m0 = 0
-        for width, per_bank in TAIL_PIECES:
+        for width, per_bank, per_store in TAIL_PIECES:
             m1 = m0 + width
             last_rows = range(ROWS - 2, ROWS)
             xa = {row: keep.tile([P, width], F32, name="xa_tail", tag=f"xa_tail{row}") for row in last_rows}
@@ -271,5 +276,5 @@ def tile_list_roost_jamming_scores_kernel(
             tile = reuse.tile([P, width, PACK], BF16, name=f"z_tail{m0}", align_bytes=64, offset=AREA_W1 + 8 * m0)
             multiply(tile, top, xb, m0, m1)
             quantise(tile, z_w[1][:, m0:m1], z_s[1][:, m0:m1])
-            scores(m0, m1, per_bank)
+            scores(m0, m1, per_bank, per_store)
             m0 = m1

@@ -20,12 +20,22 @@ P = 128
 PACK = 4
 PASS = P * PACK
 BANK = 512
+BANKS = 8
 PER_COL = 16
-RUN = 4
-AREA_WORDS, AREA_SCALES, AREA_PICKED, AREA_W1 = 0, 16384, 29824, 38016
-H_SLOTS = 8
 ROWS = H // P
+H_SLOTS = 8
+RUN = 4
 PAIR = 2
+
+AREA_WORDS = 0
+AREA_SCALES = AREA_WORDS + 4 * T
+AREA_BIASES = AREA_SCALES + H
+AREA_W2 = AREA_BIASES + 128
+AREA_W1_FIRST = AREA_SCALES + T
+AREA_PICKED = AREA_W2 + 4 * PACK * N
+AREA_W4_RAW = AREA_PICKED + 4 * BANK
+AREA_W1_LAST = AREA_PICKED + 4 * S
+
 TAIL_PIECES = ((256, 2, 6), (256, 2, 6), (256, 2, 6), (128, 3, 6), (128, 1, 2))
 
 
@@ -43,7 +53,7 @@ def tile_list_roost_jamming_scores_kernel(
 
         def next_bank(width):
             banks_used.append(width)
-            return psum.tile([P, width], F32, name="acc", tag=f"bank{len(banks_used) % 8}")
+            return psum.tile([P, width], F32, name="acc", tag=f"bank{len(banks_used) % BANKS}")
 
         def load_scale_rows(dst, src, engine):
             engine.memset(dst[:].bitcast(I32), 0)
@@ -66,24 +76,24 @@ def tile_list_roost_jamming_scores_kernel(
         tab_w = reuse.tile([P, T], U32, name="tab_w", align_bytes=64, offset=AREA_WORDS)
         tab_s = reuse.tile([P, T], U8, name="tab_s", align_bytes=64, offset=AREA_SCALES)
         w4_raw = keep.tile([P, H], U16, name="w4_raw", align_bytes=64)
-        w4s_raw = reuse.tile([P, H], U8, name="w4s_raw", align_bytes=64, offset=AREA_PICKED + 4 * BANK)
+        w4s_raw = reuse.tile([P, H], U8, name="w4s_raw", align_bytes=64, offset=AREA_W4_RAW)
         list1 = load_plain("list1", offs, U16)
         load_scale_rows(tab_s, tab_scales, nc.vector)
         list3 = load_plain("list3", offs3, U16)
-        list2 = load_plain("list2", offs2, U16)
+        gain_sb = keep.tile([P, ROWS], F32, name="gain_sb")
+        load_per_row(gain_sb, gain)
         nc.sync.dma_start(tab_w[:].bitcast(I32), tab_words[0].rearrange("p t i -> p (t i)").bitcast(I32))
         load_scale_rows(w4s_raw, w4_scales, nc.gpsimd)
-        gain_sb = keep.tile([P, ROWS], F32, name="gain_sb")
-        b4_sb = reuse.tile([P, ROWS], F32, name="b4_sb", align_bytes=64, offset=AREA_PICKED + 4 * BANK + H)
+        b4_sb = reuse.tile([P, ROWS], F32, name="b4_sb", align_bytes=64, offset=AREA_W4_RAW + H)
         b1_sb = keep.tile([P, ROWS], F32, name="b1_sb")
         nc.sync.dma_start(w4_raw[:].bitcast(I32), w4_words[0].bitcast(I32))
-        load_per_row(gain_sb, gain)
         load_per_row(b4_sb, b4)
-        w1_raw = [load_weight("w1_raw0", w1[:, 0:PASS], AREA_SCALES + T)]
-        load_per_row(b1_sb, b1)
+        w1_raw = [load_weight("w1_raw0", w1[:, 0:PASS], AREA_W1_FIRST)]
         wgb_sb = load_plain("wgb_sb", wgb, F32)
+        load_per_row(b1_sb, b1)
+        list2 = load_plain("list2", offs2, U16)
         wga_sb = load_plain("wga_sb", wga, F32)
-        w1_raw.append(load_weight("w1_raw1", w1[:, PASS : 2 * PASS], AREA_W1))
+        w1_raw.append(load_weight("w1_raw1", w1[:, PASS : 2 * PASS], AREA_W1_LAST))
         b2_sb = keep.tile([P, N // P], F32, name="b2_sb")
         with nc.allow_non_contiguous_dma(reason="one bias value a partition"):
             nc.sync.dma_start(b2_sb[:], b2.rearrange("(c p) -> p c", p=P))
@@ -94,26 +104,28 @@ def tile_list_roost_jamming_scores_kernel(
         w4_w = keep.tile([P, H], U16, name="w4_w", align_bytes=64)
         w4_s = reuse.tile([P, H], U8, name="w4_s", align_bytes=64, offset=AREA_SCALES)
 
-        def deal_w4(copy, dst, src, b):
+        def reorder_w4(copy, dst, src, b):
             cols = slice(b * PASS, (b + 1) * PASS)
-            copy(dst[:, cols].rearrange("p (i m) -> p i m", i=PACK), src[:, cols].rearrange("p (m i) -> p i m", i=PACK))
+            copy(dst[:, cols].rearrange("p (i c) -> p i c", i=PACK), src[:, cols].rearrange("p (c i) -> p i c", i=PACK))
 
         gain_sign = keep.tile([P, ROWS], F32, name="gain_sign")
         gain_size = keep.tile([P, ROWS], F32, name="gain_size")
         nc.scalar.activation(out=gain_sign[:], in_=gain_sb[:], func=ACT.Sign)
         nc.scalar.activation(out=gain_size[:], in_=gain_sb[:], func=ACT.Abs)
-        b4_signed = reuse.tile([P, ROWS], F32, name="b4_signed", align_bytes=64, offset=AREA_SCALES + H)
-        b1_sized = reuse.tile([P, ROWS], F32, name="b1_sized", align_bytes=64, offset=AREA_SCALES + H + 64)
+        b4_signed = reuse.tile([P, ROWS], F32, name="b4_signed", align_bytes=64, offset=AREA_BIASES)
+        b1_sized = reuse.tile([P, ROWS], F32, name="b1_sized", align_bytes=64, offset=AREA_BIASES + 64)
         nc.vector.tensor_tensor(b4_signed[:], b4_sb[:], gain_sign[:], ALU.mult)
         nc.vector.tensor_tensor(b1_sized[:], b1_sb[:], gain_size[:], ALU.mult)
         for b in range(2):
-            deal_w4(nc.vector.tensor_copy, w4_s, w4s_raw, b)
-            deal_w4(nc.scalar.copy, w4_w, w4_raw, b)
+            reorder_w4(nc.vector.tensor_copy, w4_s, w4s_raw, b)
+            reorder_w4(nc.scalar.copy, w4_w, w4_raw, b)
+
         v_first = reuse.tile([P, BANK], U32, name="v_first", align_bytes=64, offset=AREA_PICKED)
         v_rest = reuse.tile([P, S - BANK], U32, name="v_rest", align_bytes=64, offset=AREA_PICKED + 4 * BANK)
-        v_w = [v_first[:]] + [v_rest[:, c : c + BANK] for c in range(0, S - BANK, BANK)]
-        for c in range(S // BANK):
-            nc.vector.tensor_copy(v_w[c], tab_w[:].indirect(list1[:, c * BANK // PER_COL : (c + 1) * BANK // PER_COL]))
+        v_w = [v_first[:]] + [v_rest[:, start : start + BANK] for start in range(0, S - BANK, BANK)]
+        for chunk in range(S // BANK):
+            entries = list1[:, chunk * BANK // PER_COL : (chunk + 1) * BANK // PER_COL]
+            nc.vector.tensor_copy(v_w[chunk], tab_w[:].indirect(entries))
 
         w1_w = keep.tile([P, H], U32, name="w1_w", align_bytes=64)
         w1_s = keep.tile([P, H], U8, name="w1_s", align_bytes=64)
@@ -121,51 +133,51 @@ def tile_list_roost_jamming_scores_kernel(
         def quantise_w1(b, u, copy):
             grouped = keep.tile([P, 2, P, PACK], BF16, name=f"w1_grouped{b}{u}", align_bytes=64)
             copy(
-                grouped[:].rearrange("p i m j -> p m j i"),
-                w1_raw[b][:].rearrange("p j (m i) -> p m j i", i=PACK)[:, :, :, 2 * u : 2 * u + 2],
+                grouped[:].rearrange("p i c j -> p c j i"),
+                w1_raw[b][:].rearrange("p j (c i) -> p c j i", i=PACK)[:, :, :, 2 * u : 2 * u + 2],
             )
             cols = slice(b * PASS + 2 * u * P, b * PASS + (2 * u + 2) * P)
             nc.vector.quantize_mx(
                 out=w1_w[:, cols].bitcast(FP8X4), scales=w1_s[:, cols],
-                in_=grouped[:].rearrange("p i m j -> p (i m j)"),
+                in_=grouped[:].rearrange("p i c j -> p (i c j)"),
             )
 
-        def feature_chunk(h, side, row, c):
-            w_codes, w_scales, dtype, factor, bias = side
+        def feature_chunk(h, side, row, chunk):
+            w_codes, w_scales, dtype, factor, scaled_bias = side
             cols = slice(row * P, (row + 1) * P)
-            picked = slice(c * BANK, (c + 1) * BANK)
+            picked = slice(chunk * BANK, (chunk + 1) * BANK)
             acc = next_bank(BANK)
             nc.tensor.matmul_mx(
                 out=acc[:], lhsT=w_codes[:, cols].bitcast(dtype), lhsT_scale=w_scales[:, cols],
-                rhs=v_w[c].bitcast(FP8X4), rhs_scale=v_s[:, picked], start=True, stop=True,
+                rhs=v_w[chunk].bitcast(FP8X4), rhs_scale=v_s[:, picked], start=True, stop=True,
             )
             nc.scalar.activation(
                 out=h[:, picked], in_=acc[:], func=ACT.Identity,
-                bias=bias[:, row : row + 1], scale=factor[:, row : row + 1],
+                bias=scaled_bias[:, row : row + 1], scale=factor[:, row : row + 1],
             )
 
-        made = []
+        rows_made = []
 
         def features(side, some_rows):
             tiles = []
             for row in some_rows:
-                tiles.append(keep.tile([P, S], F32, name="h", tag=f"h{len(made) % H_SLOTS}"))
-                made.append(row)
-            for c in range(S // BANK):
+                tiles.append(keep.tile([P, S], F32, name="h", tag=f"h{len(rows_made) % H_SLOTS}"))
+                rows_made.append(row)
+            for chunk in range(S // BANK):
                 for h, row in zip(tiles, some_rows):
-                    feature_chunk(h, side, row, c)
+                    feature_chunk(h, side, row, chunk)
             return tiles
 
         jammer = (w4_w, w4_s, FP4X4, gain_sign, b4_signed)
         emitter = (w1_w, w1_s, FP8X4, gain_size, b1_sized)
 
-        def pick(dst, h, lst, wg, m0, m1):
+        def pick(dst, h, offsets, weights, m0, m1):
             nc.vector.tensor_tensor(
-                dst, h[:].indirect(lst[:, m0 // PER_COL : m1 // PER_COL]), wg[:, m0:m1], ALU.mult
+                dst, h[:].indirect(offsets[:, m0 // PER_COL : m1 // PER_COL]), weights[:, m0:m1], ALU.mult
             )
 
-        def larger(top, xa, xb, row):
-            nc.vector.scalar_tensor_tensor(top, xb, gain_sb[:, row : row + 1], xa, ALU.mult, ALU.max)
+        def larger(dst, picked_a, picked_b, row):
+            nc.vector.scalar_tensor_tensor(dst, picked_b, gain_sb[:, row : row + 1], picked_a, ALU.mult, ALU.max)
 
         z_w = [keep.tile([P, M], U32, name=f"z_w{b}", align_bytes=64) for b in range(2)]
         z_s = [keep.tile([P, M], U8, name=f"z_s{b}", align_bytes=64) for b in range(2)]
@@ -177,9 +189,9 @@ def tile_list_roost_jamming_scores_kernel(
 
         def multiply(grouped, top, xb, m0, m1):
             nc.vector.tensor_tensor(
-                grouped[:].rearrange("p (c i) j -> p c j i", i=PAIR),
-                top[:, :, m0:m1].rearrange("p j (c i) -> p c j i", i=PAIR),
-                xb[:, :, m0:m1].rearrange("p j (c i) -> p c j i", i=PAIR),
+                grouped[:].rearrange("p (c n) j -> p c j n", n=PAIR),
+                top[:, :, m0:m1].rearrange("p j (c n) -> p c j n", n=PAIR),
+                xb[:, :, m0:m1].rearrange("p j (c n) -> p c j n", n=PAIR),
                 ALU.mult,
             )
 
@@ -190,35 +202,35 @@ def tile_list_roost_jamming_scores_kernel(
             cols = slice(half * N // 2, (half + 1) * N // 2)
             grouped = keep.tile([P, N // 2, PACK], BF16, name=f"w2_grouped{b}{half}", align_bytes=64)
             nc.scalar.copy(
-                grouped[:].rearrange("p (c i) j -> p c j i", i=RUN),
-                w2_raw[b][:, :, cols].rearrange("p j (c i) -> p c j i", i=RUN),
+                grouped[:].rearrange("p (c n) j -> p c j n", n=RUN),
+                w2_raw[b][:, :, cols].rearrange("p j (c n) -> p c j n", n=RUN),
             )
             quantise(grouped, w2_w[b][:, cols], w2_s[b][:, cols])
 
         def scores(m0, m1, per_bank, per_store):
             width = m1 - m0
             staged = keep.tile([P, N // P, width], F32, name=f"staged{m0}")
-            for c0 in range(0, N // P, per_bank):
+            for first_sum in range(0, N // P, per_bank):
                 acc = next_bank(per_bank * width)
                 for b in range(2):
-                    for k in range(per_bank):
-                        cols = slice((c0 + k) * P, (c0 + k + 1) * P)
+                    for place in range(per_bank):
+                        cols = slice((first_sum + place) * P, (first_sum + place + 1) * P)
                         nc.tensor.matmul_mx(
-                            out=acc[:, k * width : (k + 1) * width],
+                            out=acc[:, place * width : (place + 1) * width],
                             lhsT=w2_w[b][:, cols].bitcast(FP8X4), lhsT_scale=w2_s[b][:, cols],
                             rhs=z_w[b][:, m0:m1].bitcast(FP8X4), rhs_scale=z_s[b][:, m0:m1],
-                            start=(b == 0 and k == 0), stop=(b == 1 and k == per_bank - 1),
+                            start=(b == 0 and place == 0), stop=(b == 1 and place == per_bank - 1),
                         )
-                for k in range(per_bank):
+                for place in range(per_bank):
                     nc.scalar.activation(
-                        out=staged[:, c0 + k, :], in_=acc[:, k * width : (k + 1) * width],
-                        func=ACT.Abs, bias=b2_sb[:, c0 + k : c0 + k + 1],
+                        out=staged[:, first_sum + place, :], in_=acc[:, place * width : (place + 1) * width],
+                        func=ACT.Abs, bias=b2_sb[:, first_sum + place : first_sum + place + 1],
                     )
-                done = c0 + per_bank
+                done = first_sum + per_bank
                 if done % per_store == 0:
-                    first = done - per_store
+                    stored = done - per_store
                     nc.sync.dma_start(
-                        out[first * P : done * P, m0:m1].rearrange("(c p) m -> p c m", p=P), staged[:, first:done, :]
+                        out[stored * P : done * P, m0:m1].rearrange("(c p) m -> p c m", p=P), staged[:, stored:done, :]
                     )
 
         quantise_w1(0, 0, nc.vector.tensor_copy)
@@ -227,19 +239,15 @@ def tile_list_roost_jamming_scores_kernel(
         w2_raw = []
         halves = [(0, M // 2), (M // 2, M)]
         for row in range(ROWS):
-            b, i = divmod(row, PACK)
+            i = row % PACK
             if 1 <= row < ROWS - 1:
                 hj.extend(features(jammer, [row + 1]))
             he.extend(features(emitter, [row]))
             if row < PACK - 1:
                 quantise_w1((row + 1) // 2, (row + 1) % 2, nc.scalar.copy)
             if row in (0, 2):
-                half = row // 2
-                w2_raw.append(
-                    load_weight(
-                        f"w2_raw{half}", w2[half * PASS : (half + 1) * PASS, :], (AREA_WORDS, AREA_SCALES + H + 128)[half]
-                    )
-                )
+                b = row // 2
+                w2_raw.append(load_weight(f"w2_raw{b}", w2[b * PASS : (b + 1) * PASS, :], (AREA_WORDS, AREA_W2)[b]))
             if i == 0:
                 xb = keep.tile([P, PACK, M], F32, name="xb", tag="xb")
                 top = keep.tile([P, PACK, M], F32, name="top", tag="top")
@@ -251,30 +259,35 @@ def tile_list_roost_jamming_scores_kernel(
                 for m0, m1 in halves:
                     larger(top[:, i, m0:m1], xa[:, m0:m1], xb[:, i, m0:m1], row)
             if row == PACK - 1:
-                grouped = [
-                    reuse.tile([P, M // 2, PACK], BF16, name=f"z_grouped{m0}", align_bytes=64, offset=AREA_W1 + 8 * m0)
+                z_halves = [
+                    reuse.tile(
+                        [P, M // 2, PACK], BF16, name=f"z_grouped{m0}", align_bytes=64,
+                        offset=AREA_W1_LAST + 2 * PACK * m0,
+                    )
                     for m0, m1 in halves
                 ]
-                for tile, (m0, m1) in zip(grouped, halves):
-                    multiply(tile, top, xb, m0, m1)
-                for tile, (m0, m1) in zip(grouped, halves):
-                    quantise(tile, z_w[0][:, m0:m1], z_s[0][:, m0:m1])
+                for z_half, (m0, m1) in zip(z_halves, halves):
+                    multiply(z_half, top, xb, m0, m1)
+                for z_half, (m0, m1) in zip(z_halves, halves):
+                    quantise(z_half, z_w[0][:, m0:m1], z_s[0][:, m0:m1])
             if row in (PACK - 1, PACK):
                 quantise_w2(0, row - PACK + 1)
         for half in range(2):
             quantise_w2(1, half)
 
         m0 = 0
+        last_rows = range(ROWS - 2, ROWS)
         for width, per_bank, per_store in TAIL_PIECES:
             m1 = m0 + width
-            last_rows = range(ROWS - 2, ROWS)
-            xa = {row: keep.tile([P, width], F32, name="xa_tail", tag=f"xa_tail{row}") for row in last_rows}
+            xa_piece = {row: keep.tile([P, width], F32, name="xa_tail", tag=f"xa_tail{row}") for row in last_rows}
             for row in last_rows:
-                pick(xa[row][:], he[row], list2, wga_sb, m0, m1)
+                pick(xa_piece[row][:], he[row], list2, wga_sb, m0, m1)
             for row in last_rows:
-                larger(top[:, row % PACK, m0:m1], xa[row][:], xb[:, row % PACK, m0:m1], row)
-            tile = reuse.tile([P, width, PACK], BF16, name=f"z_tail{m0}", align_bytes=64, offset=AREA_W1 + 8 * m0)
-            multiply(tile, top, xb, m0, m1)
-            quantise(tile, z_w[1][:, m0:m1], z_s[1][:, m0:m1])
+                larger(top[:, row % PACK, m0:m1], xa_piece[row][:], xb[:, row % PACK, m0:m1], row)
+            z_piece = reuse.tile(
+                [P, width, PACK], BF16, name=f"z_tail{m0}", align_bytes=64, offset=AREA_W1_LAST + 2 * PACK * m0
+            )
+            multiply(z_piece, top, xb, m0, m1)
+            quantise(z_piece, z_w[1][:, m0:m1], z_s[1][:, m0:m1])
             scores(m0, m1, per_bank, per_store)
             m0 = m1

from contextlib import ExitStack

import concourse.mybir as mybir

K, T, S, H, M, N = 512, 4096, 2048, 1024, 1024, 768
FLOPS = 2 * (2 * K * H * S + H * N * M)

F32 = mybir.dt.float32
BF16 = mybir.dt.bfloat16
I32 = mybir.dt.int32
U32 = mybir.dt.uint32
U16 = mybir.dt.uint16
U8 = mybir.dt.uint8
FP8X4 = mybir.dt.float8_e4m3fn_x4
FP4X4 = mybir.dt.float4_e2m1fn_x4
ALU = mybir.AluOpType
ACT = mybir.ActivationFunctionType

P = 128
PACK = 4
PASS = P * PACK
BANK = 512
BANKS = 8
PER_COL = 16
ROWS = H // P
H_SLOTS = 8
RUN = 4
PAIR = 2

AREA_WORDS = 0
AREA_SCALES = AREA_WORDS + 4 * T
AREA_BIASES = AREA_SCALES + H
AREA_W2 = AREA_BIASES + 128
AREA_W1_FIRST = AREA_SCALES + T
AREA_PICKED = AREA_W2 + 4 * PACK * N
AREA_W4_RAW = AREA_PICKED + 4 * BANK
AREA_W1_LAST = AREA_PICKED + 4 * S

TAIL_PIECES = ((256, 2, 6), (256, 2, 6), (256, 2, 6), (128, 3, 6), (128, 1, 2))


def tile_list_roost_jamming_scores_kernel(
    tc, tab_words, tab_scales, offs, offs2, offs3, w1, b1, w4_words, w4_scales, b4,
    wga, wgb, gain, w2, b2, out,
):
    nc = tc.nc
    with ExitStack() as ctx:
        keep = ctx.enter_context(tc.tile_pool(name="keep", bufs=1))
        reuse = ctx.enter_context(tc.tile_pool(name="reuse", bufs=1))
        psum = ctx.enter_context(tc.psum_pool(name="psum", bufs=1))

        banks_used = []

        def next_bank(width):
            banks_used.append(width)
            return psum.tile([P, width], F32, name="acc", tag=f"bank{len(banks_used) % BANKS}")

        def load_scale_rows(dst, src, engine):
            engine.memset(dst[:].bitcast(I32), 0)
            for q in range(4):
                nc.sync.dma_start(dst[32 * q : 32 * q + 4, :].bitcast(I32), src[0, 4 * q : 4 * q + 4, :].bitcast(I32))

        def load_plain(name, src, dtype):
            dst = keep.tile(list(src.shape), dtype, name=name)
            nc.sync.dma_start(dst[:], src)
            return dst

        def load_per_row(dst, vec):
            nc.sync.dma_start(dst[:].rearrange("p (b i) -> p b i", i=PACK), vec.rearrange("(b p i) -> p b i", p=P, i=PACK))

        def load_weight(name, rows, offset):
            raw = reuse.tile([P, PACK, rows.shape[1]], F32, name=name, align_bytes=64, offset=offset)
            nc.sync.dma_start(raw[:], rows.rearrange("(p j) c -> p j c", j=PACK))
            return raw

        tab_w = reuse.tile([P, T], U32, name="tab_w", align_bytes=64, offset=AREA_WORDS)
        tab_s = reuse.tile([P, T], U8, name="tab_s", align_bytes=64, offset=AREA_SCALES)
        w4_raw = keep.tile([P, H], U16, name="w4_raw", align_bytes=64)
        w4s_raw = reuse.tile([P, H], U8, name="w4s_raw", align_bytes=64, offset=AREA_W4_RAW)
        list1 = load_plain("list1", offs, U16)
        load_scale_rows(tab_s, tab_scales, nc.vector)
        list3 = load_plain("list3", offs3, U16)
        gain_sb = keep.tile([P, ROWS], F32, name="gain_sb")
        load_per_row(gain_sb, gain)
        nc.sync.dma_start(tab_w[:].bitcast(I32), tab_words[0].rearrange("p t i -> p (t i)").bitcast(I32))
        load_scale_rows(w4s_raw, w4_scales, nc.gpsimd)
        b4_sb = reuse.tile([P, ROWS], F32, name="b4_sb", align_bytes=64, offset=AREA_W4_RAW + H)
        b1_sb = keep.tile([P, ROWS], F32, name="b1_sb")
        nc.sync.dma_start(w4_raw[:].bitcast(I32), w4_words[0].bitcast(I32))
        load_per_row(b4_sb, b4)
        w1_raw = [load_weight("w1_raw0", w1[:, 0:PASS], AREA_W1_FIRST)]
        wgb_sb = load_plain("wgb_sb", wgb, F32)
        load_per_row(b1_sb, b1)
        list2 = load_plain("list2", offs2, U16)
        wga_sb = load_plain("wga_sb", wga, F32)
        w1_raw.append(load_weight("w1_raw1", w1[:, PASS : 2 * PASS], AREA_W1_LAST))
        b2_sb = keep.tile([P, N // P], F32, name="b2_sb")
        with nc.allow_non_contiguous_dma(reason="one bias value a partition"):
            nc.sync.dma_start(b2_sb[:], b2.rearrange("(c p) -> p c", p=P))

        v_s = keep.tile([P, S], U8, name="v_s", align_bytes=64)
        nc.vector.tensor_copy(v_s[:], tab_s[:].indirect(list1[:]))

        w4_w = keep.tile([P, H], U16, name="w4_w", align_bytes=64)
        w4_s = reuse.tile([P, H], U8, name="w4_s", align_bytes=64, offset=AREA_SCALES)

        def reorder_w4(copy, dst, src, b):
            cols = slice(b * PASS, (b + 1) * PASS)
            copy(dst[:, cols].rearrange("p (i c) -> p i c", i=PACK), src[:, cols].rearrange("p (c i) -> p i c", i=PACK))

        gain_sign = keep.tile([P, ROWS], F32, name="gain_sign")
        gain_size = keep.tile([P, ROWS], F32, name="gain_size")
        nc.scalar.activation(out=gain_sign[:], in_=gain_sb[:], func=ACT.Sign)
        nc.scalar.activation(out=gain_size[:], in_=gain_sb[:], func=ACT.Abs)
        b4_signed = reuse.tile([P, ROWS], F32, name="b4_signed", align_bytes=64, offset=AREA_BIASES)
        b1_sized = reuse.tile([P, ROWS], F32, name="b1_sized", align_bytes=64, offset=AREA_BIASES + 64)
        nc.vector.tensor_tensor(b4_signed[:], b4_sb[:], gain_sign[:], ALU.mult)
        nc.vector.tensor_tensor(b1_sized[:], b1_sb[:], gain_size[:], ALU.mult)
        for b in range(2):
            reorder_w4(nc.vector.tensor_copy, w4_s, w4s_raw, b)
            reorder_w4(nc.scalar.copy, w4_w, w4_raw, b)

        v_first = reuse.tile([P, BANK], U32, name="v_first", align_bytes=64, offset=AREA_PICKED)
        v_rest = reuse.tile([P, S - BANK], U32, name="v_rest", align_bytes=64, offset=AREA_PICKED + 4 * BANK)
        v_w = [v_first[:]] + [v_rest[:, start : start + BANK] for start in range(0, S - BANK, BANK)]
        for chunk in range(S // BANK):
            entries = list1[:, chunk * BANK // PER_COL : (chunk + 1) * BANK // PER_COL]
            nc.vector.tensor_copy(v_w[chunk], tab_w[:].indirect(entries))

        w1_w = keep.tile([P, H], U32, name="w1_w", align_bytes=64)
        w1_s = keep.tile([P, H], U8, name="w1_s", align_bytes=64)

        def quantise_w1(b, u, copy):
            grouped = keep.tile([P, 2, P, PACK], BF16, name=f"w1_grouped{b}{u}", align_bytes=64)
            copy(
                grouped[:].rearrange("p i c j -> p c j i"),
                w1_raw[b][:].rearrange("p j (c i) -> p c j i", i=PACK)[:, :, :, 2 * u : 2 * u + 2],
            )
            cols = slice(b * PASS + 2 * u * P, b * PASS + (2 * u + 2) * P)
            nc.vector.quantize_mx(
                out=w1_w[:, cols].bitcast(FP8X4), scales=w1_s[:, cols],
                in_=grouped[:].rearrange("p i c j -> p (i c j)"),
            )

        def feature_chunk(h, side, row, chunk):
            w_codes, w_scales, dtype, factor, scaled_bias = side
            cols = slice(row * P, (row + 1) * P)
            picked = slice(chunk * BANK, (chunk + 1) * BANK)
            acc = next_bank(BANK)
            nc.tensor.matmul_mx(
                out=acc[:], lhsT=w_codes[:, cols].bitcast(dtype), lhsT_scale=w_scales[:, cols],
                rhs=v_w[chunk].bitcast(FP8X4), rhs_scale=v_s[:, picked], start=True, stop=True,
            )
            nc.scalar.activation(
                out=h[:, picked], in_=acc[:], func=ACT.Identity,
                bias=scaled_bias[:, row : row + 1], scale=factor[:, row : row + 1],
            )

        rows_made = []

        def features(side, some_rows):
            tiles = []
            for row in some_rows:
                tiles.append(keep.tile([P, S], F32, name="h", tag=f"h{len(rows_made) % H_SLOTS}"))
                rows_made.append(row)
            for chunk in range(S // BANK):
                for h, row in zip(tiles, some_rows):
                    feature_chunk(h, side, row, chunk)
            return tiles

        jammer = (w4_w, w4_s, FP4X4, gain_sign, b4_signed)
        emitter = (w1_w, w1_s, FP8X4, gain_size, b1_sized)

        def pick(dst, h, offsets, weights, m0, m1):
            nc.vector.tensor_tensor(
                dst, h[:].indirect(offsets[:, m0 // PER_COL : m1 // PER_COL]), weights[:, m0:m1], ALU.mult
            )

        def larger(dst, picked_a, picked_b, row):
            nc.vector.scalar_tensor_tensor(dst, picked_b, gain_sb[:, row : row + 1], picked_a, ALU.mult, ALU.max)

        z_w = [keep.tile([P, M], U32, name=f"z_w{b}", align_bytes=64) for b in range(2)]
        z_s = [keep.tile([P, M], U8, name=f"z_s{b}", align_bytes=64) for b in range(2)]

        def quantise(grouped, codes, scales):
            nc.vector.quantize_mx(
                out=codes.bitcast(FP8X4), scales=scales, in_=grouped[:].rearrange("p c j -> p (c j)")
            )

        def multiply(grouped, top, xb, m0, m1):
            nc.vector.tensor_tensor(
                grouped[:].rearrange("p (c n) j -> p c j n", n=PAIR),
                top[:, :, m0:m1].rearrange("p j (c n) -> p c j n", n=PAIR),
                xb[:, :, m0:m1].rearrange("p j (c n) -> p c j n", n=PAIR),
                ALU.mult,
            )

        w2_w = [keep.tile([P, N], U32, name=f"w2_w{b}", align_bytes=64) for b in range(2)]
        w2_s = [keep.tile([P, N], U8, name=f"w2_s{b}", align_bytes=64) for b in range(2)]

        def quantise_w2(b, half):
            cols = slice(half * N // 2, (half + 1) * N // 2)
            grouped = keep.tile([P, N // 2, PACK], BF16, name=f"w2_grouped{b}{half}", align_bytes=64)
            nc.scalar.copy(
                grouped[:].rearrange("p (c n) j -> p c j n", n=RUN),
                w2_raw[b][:, :, cols].rearrange("p j (c n) -> p c j n", n=RUN),
            )
            quantise(grouped, w2_w[b][:, cols], w2_s[b][:, cols])

        def scores(m0, m1, per_bank, per_store):
            width = m1 - m0
            staged = keep.tile([P, N // P, width], F32, name=f"staged{m0}")
            for first_sum in range(0, N // P, per_bank):
                acc = next_bank(per_bank * width)
                for b in range(2):
                    for place in range(per_bank):
                        cols = slice((first_sum + place) * P, (first_sum + place + 1) * P)
                        nc.tensor.matmul_mx(
                            out=acc[:, place * width : (place + 1) * width],
                            lhsT=w2_w[b][:, cols].bitcast(FP8X4), lhsT_scale=w2_s[b][:, cols],
                            rhs=z_w[b][:, m0:m1].bitcast(FP8X4), rhs_scale=z_s[b][:, m0:m1],
                            start=(b == 0 and place == 0), stop=(b == 1 and place == per_bank - 1),
                        )
                for place in range(per_bank):
                    nc.scalar.activation(
                        out=staged[:, first_sum + place, :], in_=acc[:, place * width : (place + 1) * width],
                        func=ACT.Abs, bias=b2_sb[:, first_sum + place : first_sum + place + 1],
                    )
                done = first_sum + per_bank
                if done % per_store == 0:
                    stored = done - per_store
                    nc.sync.dma_start(
                        out[stored * P : done * P, m0:m1].rearrange("(c p) m -> p c m", p=P), staged[:, stored:done, :]
                    )

        quantise_w1(0, 0, nc.vector.tensor_copy)
        hj = features(jammer, [0, 1])
        he = []
        w2_raw = []
        halves = [(0, M // 2), (M // 2, M)]
        for row in range(ROWS):
            i = row % PACK
            if 1 <= row < ROWS - 1:
                hj.extend(features(jammer, [row + 1]))
            he.extend(features(emitter, [row]))
            if row < PACK - 1:
                quantise_w1((row + 1) // 2, (row + 1) % 2, nc.scalar.copy)
            if row in (0, 2):
                b = row // 2
                w2_raw.append(load_weight(f"w2_raw{b}", w2[b * PASS : (b + 1) * PASS, :], (AREA_WORDS, AREA_W2)[b]))
            if i == 0:
                xb = keep.tile([P, PACK, M], F32, name="xb", tag="xb")
                top = keep.tile([P, PACK, M], F32, name="top", tag="top")
            pick(xb[:, i, :], hj[row], list3, wgb_sb, 0, M)
            if row < ROWS - 2:
                xa = keep.tile([P, M], F32, name="xa", tag="xa")
                for m0, m1 in halves:
                    pick(xa[:, m0:m1], he[row], list2, wga_sb, m0, m1)
                for m0, m1 in halves:
                    larger(top[:, i, m0:m1], xa[:, m0:m1], xb[:, i, m0:m1], row)
            if row == PACK - 1:
                z_halves = [
                    reuse.tile(
                        [P, M // 2, PACK], BF16, name=f"z_grouped{m0}", align_bytes=64,
                        offset=AREA_W1_LAST + 2 * PACK * m0,
                    )
                    for m0, m1 in halves
                ]
                for z_half, (m0, m1) in zip(z_halves, halves):
                    multiply(z_half, top, xb, m0, m1)
                for z_half, (m0, m1) in zip(z_halves, halves):
                    quantise(z_half, z_w[0][:, m0:m1], z_s[0][:, m0:m1])
            if row in (PACK - 1, PACK):
                quantise_w2(0, row - PACK + 1)
        for half in range(2):
            quantise_w2(1, half)

        m0 = 0
        last_rows = range(ROWS - 2, ROWS)
        for width, per_bank, per_store in TAIL_PIECES:
            m1 = m0 + width
            xa_piece = {row: keep.tile([P, width], F32, name="xa_tail", tag=f"xa_tail{row}") for row in last_rows}
            for row in last_rows:
                pick(xa_piece[row][:], he[row], list2, wga_sb, m0, m1)
            for row in last_rows:
                larger(top[:, row % PACK, m0:m1], xa_piece[row][:], xb[:, row % PACK, m0:m1], row)
            z_piece = reuse.tile(
                [P, width, PACK], BF16, name=f"z_tail{m0}", align_bytes=64, offset=AREA_W1_LAST + 2 * PACK * m0
            )
            multiply(z_piece, top, xb, m0, m1)
            quantise(z_piece, z_w[1][:, m0:m1], z_s[1][:, m0:m1])
            scores(m0, m1, per_bank, per_store)
            m0 = m1
